import numpy as np
import ml_dtypes

BF16 = ml_dtypes.bfloat16


def bf(x):
    return np.asarray(x, np.float32).astype(BF16)


def f32(x):
    return np.asarray(x, np.float32)


def f64(x):
    return np.asarray(x).astype(np.float64)


def striped(idx):
    return np.tile(idx.reshape(-1, 16).T, (8, 1))


S, K, M, N, D, V = 2048, 128, 128, 1024, 2, 512


def setup_inputs():
    return {"table": bf(np.random.standard_normal((K, S))), "w": bf(np.random.standard_normal((K, M)) / np.sqrt(D * K)), "b": f32(0.5 * np.random.standard_normal((M, 1))), "offs": striped(np.random.permutation(S)[:N])}


def reference(table, w, b, offs):
    idx = offs[:16].T.reshape(-1)
    x = f64(table)[:, idx]
    y = f64(w).T @ sum(x[:, t * V : (t + 1) * V] for t in range(D))
    return np.tanh(y + f64(b))

@@ -1,0 +1,37 @@
+import concourse.mybir as mybir
+
+BF16, F32, U16 = mybir.dt.bfloat16, mybir.dt.float32, mybir.dt.uint16
+TANH = mybir.ActivationFunctionType.Tanh
+
+P = 128
+S = 2048
+V = 512
+D = 2
+PIECE = V // 16
+
+FLOPS = 2 * D * P * P * V
+
+
+def tile_gather_matmul_kernel(tc, table, w, b, offs, out):
+    nc = tc.nc
+    with (
+        tc.tile_pool(name="held", bufs=1) as held,
+        tc.psum_pool(name="psum", bufs=1) as psum,
+    ):
+        offsets = held.tile([P, D * PIECE], U16, name="offsets")
+        nodes = held.tile([P, S], BF16, name="nodes")
+        weights = held.tile([P, P], BF16, name="weights")
+        bias = held.tile([P, 1], F32, name="bias")
+        nc.sync.dma_start(nodes[:], table)
+        nc.sync.dma_start(offsets[:], offs)
+        nc.scalar.dma_start(weights[:], w)
+        nc.scalar.dma_start(bias[:], b)
+
+        y = psum.tile([P, V], F32, name="y")
+        for t in range(D):
+            neighbours = nodes[:].indirect(offsets[:, t * PIECE : (t + 1) * PIECE])
+            nc.tensor.matmul(y[:], weights[:], neighbours, start=t == 0, stop=t == D - 1)
+
+        result = held.tile([P, V], F32, name="result")
+        nc.scalar.activation(result[:], y[:], TANH, bias=bias[:])
+        nc.sync.dma_start(out, result[:])

@@ -27,6 +27,11 @@ def tile_gather_matmul_kernel(tc, table, w, b, offs, out):
         nc.scalar.dma_start(weights[:], w)
         nc.scalar.dma_start(bias[:], b)
 
+        zero = held.tile([P, 1], F32, name="zero")
+        warm = held.tile([P, 1], F32, name="warm")
+        nc.vector.memset(zero[:], 0.0)
+        nc.scalar.activation(warm[:], zero[:], TANH)
+
         y = psum.tile([P, V], F32, name="y")
         for t in range(D):
             neighbours = nodes[:].indirect(offsets[:, t * PIECE : (t + 1) * PIECE])

@@ -6,6 +6,7 @@ TANH = mybir.ActivationFunctionType.Tanh
 P = 128
 S = 2048
 V = 512
+HALF = V // 2
 D = 2
 PIECE = V // 16
 
@@ -32,11 +33,13 @@ def tile_gather_matmul_kernel(tc, table, w, b, offs, out):
         nc.vector.memset(zero[:], 0.0)
         nc.scalar.activation(warm[:], zero[:], TANH)
 
-        y = psum.tile([P, V], F32, name="y")
-        for t in range(D):
-            neighbours = nodes[:].indirect(offsets[:, t * PIECE : (t + 1) * PIECE])
-            nc.tensor.matmul(y[:], weights[:], neighbours, start=t == 0, stop=t == D - 1)
-
         result = held.tile([P, V], F32, name="result")
-        nc.scalar.activation(result[:], y[:], TANH, bias=bias[:])
-        nc.sync.dma_start(out, result[:])
+        for h in range(V // HALF):
+            y = psum.tile([P, HALF], F32, name=f"y{h}")
+            for t in range(D):
+                first = t * PIECE + h * HALF // 16
+                neighbours = nodes[:].indirect(offsets[:, first : first + HALF // 16])
+                nc.tensor.matmul(y[:], weights[:], neighbours, start=t == 0, stop=t == D - 1)
+            columns = slice(h * HALF, (h + 1) * HALF)
+            nc.scalar.activation(result[:, columns], y[:], TANH, bias=bias[:])
+            nc.sync.dma_start(out[:, columns], result[:, columns])

import concourse.mybir as mybir

BF16, F32, U16 = mybir.dt.bfloat16, mybir.dt.float32, mybir.dt.uint16
TANH = mybir.ActivationFunctionType.Tanh

P = 128
S = 2048
V = 512
HALF = V // 2
D = 2
PIECE = V // 16

FLOPS = 2 * D * P * P * V


def tile_gather_matmul_kernel(tc, table, w, b, offs, out):
    nc = tc.nc
    with (
        tc.tile_pool(name="held", bufs=1) as held,
        tc.psum_pool(name="psum", bufs=1) as psum,
    ):
        offsets = held.tile([P, D * PIECE], U16, name="offsets")
        nodes = held.tile([P, S], BF16, name="nodes")
        weights = held.tile([P, P], BF16, name="weights")
        bias = held.tile([P, 1], F32, name="bias")
        nc.sync.dma_start(nodes[:], table)
        nc.sync.dma_start(offsets[:], offs)
        nc.scalar.dma_start(weights[:], w)
        nc.scalar.dma_start(bias[:], b)

        zero = held.tile([P, 1], F32, name="zero")
        warm = held.tile([P, 1], F32, name="warm")
        nc.vector.memset(zero[:], 0.0)
        nc.scalar.activation(warm[:], zero[:], TANH)

        result = held.tile([P, V], F32, name="result")
        for h in range(V // HALF):
            y = psum.tile([P, HALF], F32, name=f"y{h}")
            for t in range(D):
                first = t * PIECE + h * HALF // 16
                neighbours = nodes[:].indirect(offsets[:, first : first + HALF // 16])
                nc.tensor.matmul(y[:], weights[:], neighbours, start=t == 0, stop=t == D - 1)
            columns = slice(h * HALF, (h + 1) * HALF)
            nc.scalar.activation(result[:, columns], y[:], TANH, bias=bias[:])
            nc.sync.dma_start(out[:, columns], result[:, columns])
